import numpy as np
import ml_dtypes


def mxq(x, axis, fmt="e4m3"):
    dtype, down = {"e4m3": (ml_dtypes.float8_e4m3fn, 7), "e5m2": (ml_dtypes.float8_e5m2, 14)}[fmt]
    v = np.moveaxis(np.asarray(x, np.float32).astype(ml_dtypes.bfloat16).astype(np.float64), axis, -1)
    blocks = v.reshape(v.shape[:-1] + (-1, 32))
    amax = np.abs(blocks).max(-1, keepdims=True)
    byte = np.maximum(np.where(amax > 0, np.frexp(amax)[1] - 1 + 127, 0) - down, 1)
    scale = np.exp2(byte - 127.0)
    codes = (blocks / scale).astype(np.float32).astype(dtype).astype(np.float64)
    return np.moveaxis((codes * scale).reshape(v.shape), -1, axis)


WIDE = False


def mx_kscale(k):
    if not WIDE:
        return np.ones(k)
    levels = np.array([18, -18])
    if k % 512:
        return np.exp2(np.random.permutation(np.resize(levels, k // 32))).repeat(32)
    a = np.empty((k // 512, 16))
    for p in range(k // 512):
        a[p, :8] = np.random.permutation(np.resize(levels, 8))
        for g in range(8):
            far = levels[np.abs(levels - a[p, g]) >= 10]
            a[p, g + 8] = far[np.random.randint(len(far))]
    return np.exp2(a.ravel()).repeat(32)


def f64(x):
    return np.asarray(x).astype(np.float64)


def striped(idx):
    return np.tile(np.asarray(idx).reshape(-1, 16).T, (8, 1)).astype(np.uint16)


def unstriped(offs):
    return offs[:16].T.reshape(-1).astype(np.int64)

def planes(y):
    n, m = y.shape
    v = y.astype(np.float32).astype(ml_dtypes.bfloat16).astype(np.float64).reshape(n // 32, 32, m)
    top = np.abs(v).max(1)
    byte = np.clip(np.where(top > 0, np.frexp(top)[1] - 1 + 127 - 7, 1), 1, 254)
    codes = (v * np.exp2(127.0 - byte)[:, None, :]).reshape(n, m).astype(np.float32).astype(ml_dtypes.float8_e4m3fn).view(np.uint8)
    words = codes.reshape(n // 512, 128, 4, m).transpose(0, 1, 3, 2)
    return np.ascontiguousarray(words), np.ascontiguousarray(byte.astype(np.uint8).reshape(n // 512, 16, m))


def setup_inputs():
    n = np.random.standard_normal
    uni = np.random.uniform
    idx = np.random.permutation(2048)[:512]
    f_d = mx_kscale(512)
    f_i = np.ones(2048)
    f_i[idx] = mx_kscale(512)
    return {
        "xT": (0.5 * n((512, 512)) * f_d[:, None]).astype(np.float32),
        "wl": (n((512, 2048)) / np.sqrt(512) / f_d[:, None] * f_i[None, :]).astype(np.float32),
        "wm": (n((512, 2048)) / np.sqrt(512) / f_d[:, None] * f_i[None, :]).astype(np.float32),
        "y": (n((512, 1))).astype(np.float32),
        "us": (uni(0.75, 1.3, (512, 1))).astype(np.float32),
        "tl": np.tile(uni(0.75, 1.3, 2048) / f_i, (128, 1)).astype(np.float32),
        "tm": np.tile(uni(0.75, 1.3, 2048) / f_i, (128, 1)).astype(np.float32),
        "wt": (uni(0.75, 1.3, (512, 1))).astype(np.float32),
        "offs": striped(idx),
    }


def reference(xT, wl, wm, y, us, tl, tm, wt, offs):
    idx = unstriped(offs)
    wl_i = f64(wl)[:, idx]
    wm_i = f64(wm)[:, idx]
    tl_i = f64(tl)[:1][:, idx]
    tm_i = f64(tm)[:1][:, idx]
    q_xT = mxq(f64(xT), 0, "e4m3")
    a = q_xT.T @ mxq(wl_i, 0, "e4m3")
    b = q_xT.T @ mxq(wm_i, 0, "e4m3")
    l = f64(us) * tl_i * a
    q = f64(us) * tm_i * b - f64(y)
    m = (l).max(-1, keepdims=True)
    e = np.exp(l - m)
    te = (e).sum(-1, keepdims=True)
    s = l - 0.5 * np.square(q)
    ms = (s).max(-1, keepdims=True)
    f = np.exp(s - ms)
    tf = (f).sum(-1, keepdims=True)
    po = f / tf
    gl = f64(wt) * f64(us) * tl_i * (e / te - po)
    gm = f64(wt) * f64(us) * tm_i * po * q
    x1 = mxq(gl, 1, "e5m2") @ mxq(wl_i, 1, "e4m3").T
    x2 = mxq(gm, 1, "e5m2") @ mxq(wm_i, 1, "e4m3").T
    out_0 = x1 + x2
    return (out_0,) + planes(out_0)

@@ -1,0 +1,287 @@
+from contextlib import ExitStack
+
+import concourse.mybir as mybir
+from concourse.masks import make_identity
+
+F32 = mybir.dt.float32
+BF16 = mybir.dt.bfloat16
+I32 = mybir.dt.int32
+U32 = mybir.dt.uint32
+U16 = mybir.dt.uint16
+U8 = mybir.dt.uint8
+E4 = mybir.dt.float8_e4m3fn_x4
+E5 = mybir.dt.float8_e5m2_x4
+ALU = mybir.AluOpType
+ACT = mybir.ActivationFunctionType
+AXIS_X = mybir.AxisListType.X
+
+P = 128
+PACK = 4
+D = 512
+R = 512
+SLOTS = 512
+POOL = 2048
+FLOPS = 4 * 2 * D * R * SLOTS
+
+
+def tile_attend_gmdn_x_pl_kernel(tc, xT, wl, wm, y, us, tl, tm, wt, offs, out_0, out_1, out_2):
+    nc = tc.nc
+    with ExitStack() as ctx:
+        sb = ctx.enter_context(tc.tile_pool(name="sb", bufs=1))
+        ps = ctx.enter_context(tc.psum_pool(name="ps", bufs=1))
+
+        def bank(tag, bufs, name):
+            return ps.tile([P, 512], F32, tag=tag, bufs=bufs, name=name)
+
+        def turn_bank(name):
+            return bank("turn", 2, name)
+
+        def score_bank(name):
+            return bank("score", 2, name)
+
+        def grad_bank(j, name):
+            return bank("grad%d" % j, 1, name)
+
+        def f32_tile(name, width=512):
+            return sb.tile([P, width], F32, name=name, align_bytes=64)
+
+        def f32_ring(tag, name):
+            return sb.tile([P, SLOTS], F32, tag=tag, bufs=2, name=name, align_bytes=64)
+
+        def bf16_tile(name, width):
+            return sb.tile([P, width], BF16, name=name, align_bytes=64)
+
+        def quantize(name, grouped, fmt):
+            width = grouped.shape[1] // PACK
+            codes = sb.tile([P, width], U32, name=name + "_codes", align_bytes=64)
+            scales = sb.tile([P, width], U8, name=name + "_scales", align_bytes=64)
+            nc.vector.quantize_mx(out=codes[:].bitcast(fmt), scales=scales[:], in_=grouped)
+            return codes, scales
+
+        offsets = sb.tile([P, SLOTS // 16], U16, name="offsets")
+        wl_rows = wl.rearrange("(p t) c -> t p c", t=PACK)
+        wm_rows = wm.rearrange("(p t) c -> t p c", t=PACK)
+        wl_win = [f32_tile("wl_win%d" % t, POOL) for t in range(PACK)]
+        wm_win = [f32_tile("wm_win%d" % t, POOL) for t in range(PACK)]
+        x_raw = f32_tile("x_raw", PACK * R)
+        tl_win = sb.tile([P, POOL], F32, tag="tl_bytes", name="tl_win", align_bytes=64)
+        tm_win = sb.tile([P, POOL], F32, tag="tm_bytes", name="tm_win", align_bytes=64)
+        nc.sync.dma_start(wl_win[0][:], wl_rows[0])
+        nc.sync.dma_start(offsets[:], offs)
+        nc.scalar.dma_start(tl_win[P - 1 : P, :], tl[0:1, :])
+        nc.scalar.dma_start(tm_win[P - 1 : P, :], tm[0:1, :])
+        row_vals = {}
+        for name, src in (("us", us), ("y", y), ("wt", wt)):
+            row_vals[name] = f32_tile(name + "_cols", PACK)
+            nc.scalar.dma_start(row_vals[name][:], src.rearrange("(s j) o -> s (j o)", j=PACK))
+        us_c, y_c, wt_c = row_vals["us"], row_vals["y"], row_vals["wt"]
+        for t in range(1, PACK):
+            nc.sync.dma_start(wl_win[t][:], wl_rows[t])
+        nc.sync.dma_start(x_raw[:], xT.rearrange("(p t) r -> p (t r)", t=PACK))
+        for t in range(PACK):
+            nc.sync.dma_start(wm_win[t][:], wm_rows[t])
+
+        ident = f32_tile("ident", P)
+        make_identity(nc, ident[:])
+        nc.vector.memset(tl_win[0 : P - 1, :], 0.0)
+        nc.gpsimd.memset(tm_win[0 : P - 1, :], 0.0)
+
+        def negated(name, src):
+            neg = f32_tile(name, PACK)
+            nc.scalar.activation(neg[:], src, ACT.Copy, scale=-1.0)
+            return neg
+
+        neg_us = negated("neg_us", us_c[:])
+        neg_y = negated("neg_y", y_c[:])
+        wu = f32_tile("wu", PACK)
+        nc.vector.tensor_tensor(wu[:], wt_c[:], us_c[:], ALU.mult)
+        neg_wu = negated("neg_wu", wu[:])
+
+        def gather_scales(name, window):
+            picked = f32_tile(name + "_picked")
+            nc.vector.tensor_copy(picked[:], window[:].indirect(offsets[:]))
+            return picked
+
+        def turn_scales(name, blocks):
+            turned = turn_bank(name + "_turned")
+            for u in range(PACK):
+                nc.tensor.transpose(turned[:, u * P : (u + 1) * P], blocks[u], ident[:])
+            return turned[:, P - 1 : PACK * P : P]
+
+        def gather_planes(name, windows):
+            planes = bf16_tile(name + "_planes", PACK * SLOTS)
+            for t in range(PACK):
+                nc.vector.tensor_copy(planes[:, t * SLOTS : (t + 1) * SLOTS], windows[t][:].indirect(offsets[:]))
+            return planes
+
+        def quantize_along_d(name, planes, vector_share):
+            grouped = bf16_tile(name + "_by_d", PACK * SLOTS)
+            dst = grouped[:].rearrange("p (c i t) -> p c t i", i=4, t=PACK)
+            src = planes[:].rearrange("p (t c i) -> p c t i", i=4, t=PACK)
+            if vector_share:
+                nc.vector.tensor_copy(dst[:, :vector_share], src[:, :vector_share])
+            nc.scalar.copy(dst[:, vector_share:], src[:, vector_share:])
+            return quantize(name + "_d", grouped[:], E4)
+
+        def quantize_along_slots(name, planes):
+            words = planes[:].bitcast(F32)
+            half = SLOTS // 2
+            grouped = bf16_tile(name + "_by_slot", PACK * D)
+            grouped_words = grouped[:].bitcast(F32).rearrange("s (p h k) -> s p h k", h=2, k=4)
+            for h in range(2):
+                turned = turn_bank("%s_turned%d" % (name, h))
+                for k in range(4):
+                    t, v = 2 * h + k // 2, k % 2
+                    nc.tensor.transpose(
+                        turned[:, k * P : (k + 1) * P], words[:, t * half + v : (t + 1) * half : 2], ident[:]
+                    )
+                nc.scalar.copy(grouped_words[:, :, h, :], turned[:].rearrange("s (k p) -> s p k", k=4))
+            return quantize(name + "_i", grouped[:], E4)
+
+        tl_picked = gather_scales("tl", tl_win)
+        tl_cols = f32_tile("tl_cols", PACK)
+        nc.scalar.copy(tl_cols[:], turn_scales("tl_runs", [tl_picked[:, k * P : (k + 1) * P] for k in range(PACK)]))
+        neg_tl_dealt = negated("neg_tl_dealt", turn_scales("tl_dealt", [tl_picked[:, u:SLOTS:PACK] for u in range(PACK)]))
+        wl_planes = gather_planes("wl", wl_win)
+
+        tm_picked = gather_scales("tm", tm_win)
+        tm_cols = f32_tile("tm_cols", PACK)
+        nc.scalar.copy(tm_cols[:], turn_scales("tm_runs", [tm_picked[:, k * P : (k + 1) * P] for k in range(PACK)]))
+        tm_spread = turn_bank("tm_spread")
+        for k in range(PACK):
+            nc.tensor.transpose(tm_spread[:, k * P : (k + 1) * P], tm_cols[:, k : k + 1].to_broadcast([P, P]), ident[:])
+        tm_rows = f32_tile("tm_rows")
+        nc.scalar.copy(tm_rows[:], tm_spread[:])
+
+        wl_d_codes, wl_d_scales = quantize_along_d("wl", wl_planes, 0)
+
+        x_grouped = bf16_tile("x_grouped", PACK * R)
+        nc.vector.tensor_copy(
+            x_grouped[:].rearrange("p (j s t) -> p s t j", j=PACK, t=PACK),
+            x_raw[:].rearrange("p (t s j) -> p s t j", j=PACK, t=PACK),
+        )
+        x_codes, x_scales = quantize("x", x_grouped[:], E4)
+
+        wm_planes = gather_planes("wm", wm_win)
+        wm_d_codes, wm_d_scales = quantize_along_d("wm", wm_planes, 88)
+
+        def scores(name, tile, stationary, moving):
+            acc = score_bank(name)
+            cols = slice(tile * P, (tile + 1) * P)
+            nc.tensor.matmul_mx(
+                out=acc[:],
+                lhsT=stationary[0][:, cols].bitcast(E4),
+                lhsT_scale=stationary[1][:, cols],
+                rhs=moving[0][:].bitcast(E4),
+                rhs_scale=moving[1][:],
+                start=True,
+                stop=True,
+            )
+            return acc
+
+        def exp_and_factor(name, neg_logits, neg_max, weight):
+            expd = f32_tile(name + "_exp")
+            total = f32_tile(name + "_sum", 1)
+            nc.scalar.activation(expd[:], neg_logits[:], ACT.Exp, bias=neg_max[:], scale=-1.0, accum_out=total[:])
+            inv = f32_tile(name + "_inv", 1)
+            nc.vector.reciprocal(inv[:], total[:])
+            factor = f32_tile(name + "_factor", 1)
+            nc.vector.tensor_scalar(factor[:], inv[:], weight, None, ALU.mult)
+            return expd, factor
+
+        def add_turned(dealt, acc, expd, factor, first):
+            nc.scalar.activation(
+                dealt[:].rearrange("r (u s) -> r s u", u=PACK),
+                expd[:].rearrange("r (s u) -> r s u", u=PACK),
+                ACT.Copy,
+                scale=factor[:],
+            )
+            for u in range(PACK):
+                nc.tensor.matmul(
+                    acc[:, u * P : (u + 1) * P],
+                    dealt[:, u * P : (u + 1) * P],
+                    ident[:],
+                    is_transpose=True,
+                    start=(first and u == 0),
+                    stop=(not first and u == PACK - 1),
+                )
+
+        scaled_a = sb.tile([P, PACK * R], F32, tag="tl_bytes", name="scaled_a", align_bytes=64)
+        for k in range(PACK):
+            a_turned = scores("a%d" % k, k, (wl_d_codes, wl_d_scales), (x_codes, x_scales))
+            nc.scalar.activation(scaled_a[:, k * R : (k + 1) * R], a_turned[:], ACT.Copy, scale=tl_cols[:, k : k + 1])
+        neg_logits, priors = [], []
+        for j in range(PACK):
+            a_rows = turn_bank("a_rows%d" % j)
+            for k in range(PACK):
+                nc.tensor.transpose(a_rows[:, k * P : (k + 1) * P], scaled_a[:, k * R + j * P : k * R + (j + 1) * P], ident[:])
+            neg_l = f32_tile("neg_l%d" % j)
+            neg_m = f32_tile("neg_m%d" % j, 1)
+            nc.vector.tensor_scalar(neg_l[:], a_rows[:], neg_us[:, j : j + 1], None, ALU.mult, ALU.min, accum_out=neg_m[:])
+            neg_logits.append(neg_l)
+            priors.append(exp_and_factor("prior%d" % j, neg_l, neg_m, neg_wu[:, j : j + 1]))
+
+        wl_i_codes, wl_i_scales = quantize_along_slots("wl", wl_planes)
+        wm_i_codes, wm_i_scales = quantize_along_slots("wm", wm_planes)
+
+        result = sb.tile([P, PACK * D], F32, tag="tm_bytes", name="result", align_bytes=64)
+        out_rows = out_0.rearrange("(s j) d -> j s d", j=PACK)
+        for j in range(PACK):
+            b = scores("b%d" % j, j, (x_codes, x_scales), (wm_d_codes, wm_d_scales))
+            mean = f32_tile("mean%d" % j)
+            nc.vector.scalar_tensor_tensor(mean[:], b[:], us_c[:, j : j + 1], tm_rows[:], ALU.mult, ALU.mult)
+            q_sq = f32_ring("q_sq", "q_sq%d" % j)
+            nc.scalar.activation(q_sq[:], mean[:], ACT.Square, bias=neg_y[:, j : j + 1])
+            neg_s = f32_tile("neg_s%d" % j)
+            nc.vector.scalar_tensor_tensor(neg_s[:], q_sq[:], 0.5, neg_logits[j][:], ALU.mult, ALU.add)
+            neg_ms = f32_tile("neg_ms%d" % j, 1)
+            nc.vector.tensor_reduce(neg_ms[:], neg_s[:], AXIS_X, ALU.min)
+            f, c2 = exp_and_factor("post%d" % j, neg_s, neg_ms, wu[:, j : j + 1])
+            diff = grad_bank(j, "diff%d" % j)
+            add_turned(f32_tile("prior_dealt%d" % j), diff, priors[j][0], priors[j][1], True)
+            add_turned(f32_ring("post_dealt", "post_dealt%d" % j), diff, f, c2, False)
+            q_tm = f32_tile("q_tm%d" % j)
+            nc.vector.scalar_tensor_tensor(q_tm[:], mean[:], neg_y[:, j : j + 1], tm_rows[:], ALU.add, ALU.mult)
+            gm = bf16_tile("gm%d" % j, SLOTS)
+            nc.vector.scalar_tensor_tensor(gm[:], f[:], c2[:], q_tm[:], ALU.mult, ALU.mult)
+            gm_turned = turn_bank("gm_turned%d" % j)
+            for v in range(2):
+                nc.tensor.transpose(gm_turned[:, v * P : (v + 1) * P], gm[:].bitcast(F32)[:, v : SLOTS // 2 : 2], ident[:])
+            grads = bf16_tile("grads%d" % j, 2 * SLOTS)
+            nc.vector.tensor_tensor(
+                grads[:, 0:SLOTS].rearrange("s (r u) -> s r u", u=PACK),
+                diff[:].rearrange("s (u r) -> s r u", u=PACK),
+                neg_tl_dealt[:].unsqueeze(1).to_broadcast([P, P, PACK]),
+                ALU.mult,
+            )
+            nc.scalar.copy(
+                grads[:].bitcast(F32)[:, SLOTS // 2 : SLOTS].rearrange("s (r v) -> s r v", v=2),
+                gm_turned[:, 0 : 2 * P].rearrange("s (v r) -> s r v", v=2),
+            )
+            g_codes, g_scales = quantize("grads%d" % j, grads[:], E5)
+            acc = grad_bank(j, "x%d" % j)
+            for n, (codes, scales) in enumerate(((wl_i_codes, wl_i_scales), (wm_i_codes, wm_i_scales))):
+                nc.tensor.matmul_mx(
+                    out=acc[:],
+                    lhsT=g_codes[:, n * P : (n + 1) * P].bitcast(E5),
+                    lhsT_scale=g_scales[:, n * P : (n + 1) * P],
+                    rhs=codes[:].bitcast(E4),
+                    rhs_scale=scales[:],
+                    start=(n == 0),
+                    stop=(n == 1),
+                )
+            nc.scalar.copy(result[:, j * D : (j + 1) * D], acc[:])
+            nc.sync.dma_start(out_rows[j], result[:, j * D : (j + 1) * D])
+
+        result_grouped = bf16_tile("result_grouped", PACK * D)
+        dst = result_grouped[:].rearrange("p (c i j) -> p c j i", i=4, j=PACK)
+        src = result[:].rearrange("p (j c i) -> p c j i", i=4, j=PACK)
+        nc.vector.tensor_copy(dst[:, :96], src[:, :96])
+        nc.scalar.copy(dst[:, 96:], src[:, 96:])
+        r_codes, r_scales = quantize("result", result_grouped[:], E4)
+        nc.sync.dma_start(out_1[0].rearrange("p c l -> p (c l)").bitcast(I32), r_codes[:].bitcast(I32))
+        for quad in range(4):
+            queue = nc.scalar if quad % 2 else nc.sync
+            queue.dma_start(
+                out_2[0, 4 * quad : 4 * quad + 4, :].bitcast(I32), r_scales[32 * quad : 32 * quad + 4, :].bitcast(I32)
+            )

@@ -62,28 +62,29 @@ def tile_attend_gmdn_x_pl_kernel(tc, xT, wl, wm, y, us, tl, tm, wt, offs, out_0,
         wl_rows = wl.rearrange("(p t) c -> t p c", t=PACK)
         wm_rows = wm.rearrange("(p t) c -> t p c", t=PACK)
         wl_win = [f32_tile("wl_win%d" % t, POOL) for t in range(PACK)]
-        wm_win = [f32_tile("wm_win%d" % t, POOL) for t in range(PACK)]
+        wm_win = [
+            sb.tile([P, POOL], F32, tag="wm_bytes%d" % t, name="wm_win%d" % t, align_bytes=64) for t in range(PACK)
+        ]
         x_raw = f32_tile("x_raw", PACK * R)
         tl_win = sb.tile([P, POOL], F32, tag="tl_bytes", name="tl_win", align_bytes=64)
         tm_win = sb.tile([P, POOL], F32, tag="tm_bytes", name="tm_win", align_bytes=64)
-        nc.sync.dma_start(wl_win[0][:], wl_rows[0])
         nc.sync.dma_start(offsets[:], offs)
-        nc.scalar.dma_start(tl_win[P - 1 : P, :], tl[0:1, :])
-        nc.scalar.dma_start(tm_win[P - 1 : P, :], tm[0:1, :])
+        nc.sync.dma_start(tl_win[P - 1 : P, :], tl[0:1, :])
+        nc.sync.dma_start(tm_win[P - 1 : P, :], tm[0:1, :])
         row_vals = {}
         for name, src in (("us", us), ("y", y), ("wt", wt)):
             row_vals[name] = f32_tile(name + "_cols", PACK)
             nc.scalar.dma_start(row_vals[name][:], src.rearrange("(s j) o -> s (j o)", j=PACK))
         us_c, y_c, wt_c = row_vals["us"], row_vals["y"], row_vals["wt"]
-        for t in range(1, PACK):
-            nc.sync.dma_start(wl_win[t][:], wl_rows[t])
         nc.sync.dma_start(x_raw[:], xT.rearrange("(p t) r -> p (t r)", t=PACK))
+        for t in range(PACK):
+            nc.sync.dma_start(wl_win[t][:], wl_rows[t])
         for t in range(PACK):
             nc.sync.dma_start(wm_win[t][:], wm_rows[t])
 
         ident = f32_tile("ident", P)
         make_identity(nc, ident[:])
-        nc.vector.memset(tl_win[0 : P - 1, :], 0.0)
+        nc.vector.memset(tl_win[0 : P - 1, :].bitcast(I32), 0)
         nc.gpsimd.memset(tm_win[0 : P - 1, :], 0.0)
 
         def negated(name, src):
@@ -142,7 +143,6 @@ def tile_attend_gmdn_x_pl_kernel(tc, xT, wl, wm, y, us, tl, tm, wt, offs, out_0,
         tl_cols = f32_tile("tl_cols", PACK)
         nc.scalar.copy(tl_cols[:], turn_scales("tl_runs", [tl_picked[:, k * P : (k + 1) * P] for k in range(PACK)]))
         neg_tl_dealt = negated("neg_tl_dealt", turn_scales("tl_dealt", [tl_picked[:, u:SLOTS:PACK] for u in range(PACK)]))
-        wl_planes = gather_planes("wl", wl_win)
 
         tm_picked = gather_scales("tm", tm_win)
         tm_cols = f32_tile("tm_cols", PACK)
@@ -153,8 +153,6 @@ def tile_attend_gmdn_x_pl_kernel(tc, xT, wl, wm, y, us, tl, tm, wt, offs, out_0,
         tm_rows = f32_tile("tm_rows")
         nc.scalar.copy(tm_rows[:], tm_spread[:])
 
-        wl_d_codes, wl_d_scales = quantize_along_d("wl", wl_planes, 0)
-
         x_grouped = bf16_tile("x_grouped", PACK * R)
         nc.vector.tensor_copy(
             x_grouped[:].rearrange("p (j s t) -> p s t j", j=PACK, t=PACK),
@@ -162,39 +160,33 @@ def tile_attend_gmdn_x_pl_kernel(tc, xT, wl, wm, y, us, tl, tm, wt, offs, out_0,
         )
         x_codes, x_scales = quantize("x", x_grouped[:], E4)
 
+        wl_planes = gather_planes("wl", wl_win)
+        wl_d_codes, wl_d_scales = quantize_along_d("wl", wl_planes, 80)
+        wl_i_codes, wl_i_scales = quantize_along_slots("wl", wl_planes)
+
         wm_planes = gather_planes("wm", wm_win)
-        wm_d_codes, wm_d_scales = quantize_along_d("wm", wm_planes, 88)
+        wm_d_codes, wm_d_scales = quantize_along_d("wm", wm_planes, 80)
 
-        def scores(name, tile, stationary, moving):
-            acc = score_bank(name)
-            cols = slice(tile * P, (tile + 1) * P)
+        def mx_pass(acc, stationary, stationary_cols, stationary_fmt, moving, moving_cols, start, stop):
             nc.tensor.matmul_mx(
-                out=acc[:],
-                lhsT=stationary[0][:, cols].bitcast(E4),
-                lhsT_scale=stationary[1][:, cols],
-                rhs=moving[0][:].bitcast(E4),
-                rhs_scale=moving[1][:],
-                start=True,
-                stop=True,
+                out=acc,
+                lhsT=stationary[0][:, stationary_cols].bitcast(stationary_fmt),
+                lhsT_scale=stationary[1][:, stationary_cols],
+                rhs=moving[0][:, moving_cols].bitcast(E4),
+                rhs_scale=moving[1][:, moving_cols],
+                start=start,
+                stop=stop,
             )
-            return acc
 
-        def exp_and_factor(name, neg_logits, neg_max, weight):
-            expd = f32_tile(name + "_exp")
-            total = f32_tile(name + "_sum", 1)
-            nc.scalar.activation(expd[:], neg_logits[:], ACT.Exp, bias=neg_max[:], scale=-1.0, accum_out=total[:])
-            inv = f32_tile(name + "_inv", 1)
-            nc.vector.reciprocal(inv[:], total[:])
-            factor = f32_tile(name + "_factor", 1)
-            nc.vector.tensor_scalar(factor[:], inv[:], weight, None, ALU.mult)
-            return expd, factor
+        def block(n):
+            return slice(n * P, (n + 1) * P)
 
         def add_turned(dealt, acc, expd, factor, first):
             nc.scalar.activation(
                 dealt[:].rearrange("r (u s) -> r s u", u=PACK),
                 expd[:].rearrange("r (s u) -> r s u", u=PACK),
                 ACT.Copy,
-                scale=factor[:],
+                scale=factor,
             )
             for u in range(PACK):
                 nc.tensor.matmul(
@@ -206,72 +198,99 @@ def tile_attend_gmdn_x_pl_kernel(tc, xT, wl, wm, y, us, tl, tm, wt, offs, out_0,
                     stop=(not first and u == PACK - 1),
                 )
 
+        x_q = (x_codes, x_scales)
+        everything = slice(0, SLOTS)
         scaled_a = sb.tile([P, PACK * R], F32, tag="tl_bytes", name="scaled_a", align_bytes=64)
-        for k in range(PACK):
-            a_turned = scores("a%d" % k, k, (wl_d_codes, wl_d_scales), (x_codes, x_scales))
-            nc.scalar.activation(scaled_a[:, k * R : (k + 1) * R], a_turned[:], ACT.Copy, scale=tl_cols[:, k : k + 1])
-        neg_logits, priors = [], []
+        neg_l_pairs = [
+            sb.tile([P, 2 * SLOTS], F32, tag="wm_bytes%d" % (2 * h + 1), name="neg_l%d" % h, align_bytes=64)
+            for h in range(2)
+        ]
+        prior_sums = f32_tile("prior_sums", PACK)
+        neg_logits, prior_exps = [], []
         for j in range(PACK):
+            a_turned = score_bank("a%d" % j)
+            for k in range(PACK):
+                mx_pass(a_turned[:, block(k)], (wl_d_codes, wl_d_scales), block(k), E4, x_q, block(j), True, True)
             a_rows = turn_bank("a_rows%d" % j)
             for k in range(PACK):
-                nc.tensor.transpose(a_rows[:, k * P : (k + 1) * P], scaled_a[:, k * R + j * P : k * R + (j + 1) * P], ident[:])
-            neg_l = f32_tile("neg_l%d" % j)
+                piece = scaled_a[:, block(PACK * j + k)]
+                nc.scalar.activation(piece, a_turned[:, block(k)], ACT.Copy, scale=tl_cols[:, k : k + 1])
+                nc.tensor.transpose(a_rows[:, block(k)], piece, ident[:])
+            neg_l = neg_l_pairs[j // 2][:, (j % 2) * SLOTS : (j % 2 + 1) * SLOTS]
             neg_m = f32_tile("neg_m%d" % j, 1)
-            nc.vector.tensor_scalar(neg_l[:], a_rows[:], neg_us[:, j : j + 1], None, ALU.mult, ALU.min, accum_out=neg_m[:])
+            nc.vector.tensor_scalar(neg_l, a_rows[:], neg_us[:, j : j + 1], None, ALU.mult, ALU.min, accum_out=neg_m[:])
+            e = f32_tile("prior_exp%d" % j)
+            nc.scalar.activation(e[:], neg_l, ACT.Exp, bias=neg_m[:], scale=-1.0, accum_out=prior_sums[:, j : j + 1])
             neg_logits.append(neg_l)
-            priors.append(exp_and_factor("prior%d" % j, neg_l, neg_m, neg_wu[:, j : j + 1]))
+            prior_exps.append(e)
+        prior_inv = f32_tile("prior_inv", PACK)
+        nc.vector.reciprocal(prior_inv[:], prior_sums[:])
+        neg_c1 = f32_tile("neg_c1", PACK)
+        nc.vector.tensor_tensor(neg_c1[:], prior_inv[:], neg_wu[:], ALU.mult)
 
-        wl_i_codes, wl_i_scales = quantize_along_slots("wl", wl_planes)
         wm_i_codes, wm_i_scales = quantize_along_slots("wm", wm_planes)
 
         result = sb.tile([P, PACK * D], F32, tag="tm_bytes", name="result", align_bytes=64)
         out_rows = out_0.rearrange("(s j) d -> j s d", j=PACK)
-        for j in range(PACK):
-            b = scores("b%d" % j, j, (x_codes, x_scales), (wm_d_codes, wm_d_scales))
-            mean = f32_tile("mean%d" % j)
-            nc.vector.scalar_tensor_tensor(mean[:], b[:], us_c[:, j : j + 1], tm_rows[:], ALU.mult, ALU.mult)
+        mean, post_exp, post_sum, c2, diff, q_tm, grads = {}, {}, {}, {}, {}, {}, {}
+
+        def posterior(j):
+            b = score_bank("b%d" % j)
+            mx_pass(b[:], x_q, block(j), E4, (wm_d_codes, wm_d_scales), everything, True, True)
+            mean[j] = f32_tile("mean%d" % j)
+            nc.vector.scalar_tensor_tensor(mean[j][:], b[:], us_c[:, j : j + 1], tm_rows[:], ALU.mult, ALU.mult)
             q_sq = f32_ring("q_sq", "q_sq%d" % j)
-            nc.scalar.activation(q_sq[:], mean[:], ACT.Square, bias=neg_y[:, j : j + 1])
+            nc.scalar.activation(q_sq[:], mean[j][:], ACT.Square, bias=neg_y[:, j : j + 1])
             neg_s = f32_tile("neg_s%d" % j)
-            nc.vector.scalar_tensor_tensor(neg_s[:], q_sq[:], 0.5, neg_logits[j][:], ALU.mult, ALU.add)
+            nc.vector.scalar_tensor_tensor(neg_s[:], q_sq[:], 0.5, neg_logits[j], ALU.mult, ALU.add)
             neg_ms = f32_tile("neg_ms%d" % j, 1)
             nc.vector.tensor_reduce(neg_ms[:], neg_s[:], AXIS_X, ALU.min)
-            f, c2 = exp_and_factor("post%d" % j, neg_s, neg_ms, wu[:, j : j + 1])
-            diff = grad_bank(j, "diff%d" % j)
-            add_turned(f32_tile("prior_dealt%d" % j), diff, priors[j][0], priors[j][1], True)
-            add_turned(f32_ring("post_dealt", "post_dealt%d" % j), diff, f, c2, False)
-            q_tm = f32_tile("q_tm%d" % j)
-            nc.vector.scalar_tensor_tensor(q_tm[:], mean[:], neg_y[:, j : j + 1], tm_rows[:], ALU.add, ALU.mult)
+            post_exp[j] = f32_tile("post_exp%d" % j)
+            post_sum[j] = f32_tile("post_sum%d" % j, 1)
+            nc.scalar.activation(post_exp[j][:], neg_s[:], ACT.Exp, bias=neg_ms[:], scale=-1.0, accum_out=post_sum[j][:])
+            diff[j] = grad_bank(j, "diff%d" % j)
+            add_turned(f32_tile("prior_dealt%d" % j), diff[j], prior_exps[j], neg_c1[:, j : j + 1], True)
+
+        def normalise(j):
+            inv = f32_tile("post_inv%d" % j, 1)
+            nc.vector.reciprocal(inv[:], post_sum[j][:])
+            c2[j] = f32_tile("c2_%d" % j, 1)
+            nc.scalar.activation(c2[j][:], inv[:], ACT.Copy, scale=wu[:, j : j + 1])
+            add_turned(f32_ring("post_dealt", "post_dealt%d" % j), diff[j], post_exp[j], c2[j][:], False)
+            q_tm[j] = f32_tile("q_tm%d" % j)
+            nc.vector.scalar_tensor_tensor(q_tm[j][:], mean[j][:], neg_y[:, j : j + 1], tm_rows[:], ALU.add, ALU.mult)
+
+        def gradients(j):
             gm = bf16_tile("gm%d" % j, SLOTS)
-            nc.vector.scalar_tensor_tensor(gm[:], f[:], c2[:], q_tm[:], ALU.mult, ALU.mult)
+            nc.vector.scalar_tensor_tensor(gm[:], post_exp[j][:], c2[j][:], q_tm[j][:], ALU.mult, ALU.mult)
             gm_turned = turn_bank("gm_turned%d" % j)
             for v in range(2):
-                nc.tensor.transpose(gm_turned[:, v * P : (v + 1) * P], gm[:].bitcast(F32)[:, v : SLOTS // 2 : 2], ident[:])
-            grads = bf16_tile("grads%d" % j, 2 * SLOTS)
+                nc.tensor.transpose(gm_turned[:, block(v)], gm[:].bitcast(F32)[:, v : SLOTS // 2 : 2], ident[:])
+            grads[j] = bf16_tile("grads%d" % j, 2 * SLOTS)
+            nc.scalar.copy(
+                grads[j][:].bitcast(F32)[:, SLOTS // 2 : SLOTS].rearrange("s (r v) -> s r v", v=2),
+                gm_turned[:, 0 : 2 * P].rearrange("s (v r) -> s r v", v=2),
+            )
             nc.vector.tensor_tensor(
-                grads[:, 0:SLOTS].rearrange("s (r u) -> s r u", u=PACK),
-                diff[:].rearrange("s (u r) -> s r u", u=PACK),
+                grads[j][:, 0:SLOTS].rearrange("s (r u) -> s r u", u=PACK),
+                diff[j][:].rearrange("s (u r) -> s r u", u=PACK),
                 neg_tl_dealt[:].unsqueeze(1).to_broadcast([P, P, PACK]),
                 ALU.mult,
             )
-            nc.scalar.copy(
-                grads[:].bitcast(F32)[:, SLOTS // 2 : SLOTS].rearrange("s (r v) -> s r v", v=2),
-                gm_turned[:, 0 : 2 * P].rearrange("s (v r) -> s r v", v=2),
-            )
-            g_codes, g_scales = quantize("grads%d" % j, grads[:], E5)
+
+        def back_product(j):
+            g_q = quantize("grads%d" % j, grads[j][:], E5)
             acc = grad_bank(j, "x%d" % j)
-            for n, (codes, scales) in enumerate(((wl_i_codes, wl_i_scales), (wm_i_codes, wm_i_scales))):
-                nc.tensor.matmul_mx(
-                    out=acc[:],
-                    lhsT=g_codes[:, n * P : (n + 1) * P].bitcast(E5),
-                    lhsT_scale=g_scales[:, n * P : (n + 1) * P],
-                    rhs=codes[:].bitcast(E4),
-                    rhs_scale=scales[:],
-                    start=(n == 0),
-                    stop=(n == 1),
-                )
+            mx_pass(acc[:], g_q, block(0), E5, (wl_i_codes, wl_i_scales), everything, True, False)
+            mx_pass(acc[:], g_q, block(1), E5, (wm_i_codes, wm_i_scales), everything, False, True)
             nc.scalar.copy(result[:, j * D : (j + 1) * D], acc[:])
             nc.sync.dma_start(out_rows[j], result[:, j * D : (j + 1) * D])
+
+        stages = (posterior, normalise, gradients, back_product)
+        for step in range(PACK + len(stages) - 1):
+            for lag, stage in enumerate(stages):
+                if 0 <= step - lag < PACK:
+                    stage(step - lag)
 
         result_grouped = bf16_tile("result_grouped", PACK * D)
         dst = result_grouped[:].rearrange("p (c i j) -> p c j i", i=4, j=PACK)

@@ -9,8 +9,8 @@ I32 = mybir.dt.int32
 U32 = mybir.dt.uint32
 U16 = mybir.dt.uint16
 U8 = mybir.dt.uint8
-E4 = mybir.dt.float8_e4m3fn_x4
-E5 = mybir.dt.float8_e5m2_x4
+E4M3 = mybir.dt.float8_e4m3fn_x4
+E5M2 = mybir.dt.float8_e5m2_x4
 ALU = mybir.AluOpType
 ACT = mybir.ActivationFunctionType
 AXIS_X = mybir.AxisListType.X
@@ -21,7 +21,15 @@ D = 512
 R = 512
 SLOTS = 512
 POOL = 2048
+BANK = 512
+RUN = 4
+TABLE_RUNS_ON_VECTOR = 80
+RESULT_RUNS_ON_VECTOR = 96
 FLOPS = 4 * 2 * D * R * SLOTS
+
+
+def block(n, count=1):
+    return slice(n * P, (n + count) * P)
 
 
 def tile_attend_gmdn_x_pl_kernel(tc, xT, wl, wm, y, us, tl, tm, wt, offs, out_0, out_1, out_2):
@@ -30,20 +38,20 @@ def tile_attend_gmdn_x_pl_kernel(tc, xT, wl, wm, y, us, tl, tm, wt, offs, out_0,
         sb = ctx.enter_context(tc.tile_pool(name="sb", bufs=1))
         ps = ctx.enter_context(tc.psum_pool(name="ps", bufs=1))
 
-        def bank(tag, bufs, name):
-            return ps.tile([P, 512], F32, tag=tag, bufs=bufs, name=name)
-
         def turn_bank(name):
-            return bank("turn", 2, name)
+            return ps.tile([P, BANK], F32, tag="turn", bufs=2, name=name)
 
         def score_bank(name):
-            return bank("score", 2, name)
+            return ps.tile([P, BANK], F32, tag="score", bufs=2, name=name)
 
-        def grad_bank(j, name):
-            return bank("grad%d" % j, 1, name)
+        def row_bank(j, name):
+            return ps.tile([P, BANK], F32, tag="row%d" % j, bufs=1, name=name)
 
-        def f32_tile(name, width=512):
+        def f32_tile(name, width):
             return sb.tile([P, width], F32, name=name, align_bytes=64)
+
+        def f32_on(tag, name, width):
+            return sb.tile([P, width], F32, tag=tag, name=name, align_bytes=64)
 
         def f32_ring(tag, name):
             return sb.tile([P, SLOTS], F32, tag=tag, bufs=2, name=name, align_bytes=64)
@@ -58,24 +66,37 @@ def tile_attend_gmdn_x_pl_kernel(tc, xT, wl, wm, y, us, tl, tm, wt, offs, out_0,
             nc.vector.quantize_mx(out=codes[:].bitcast(fmt), scales=scales[:], in_=grouped)
             return codes, scales
 
+        def mx_pass(acc, stationary, stationary_cols, stationary_fmt, moving, moving_cols, start, stop):
+            nc.tensor.matmul_mx(
+                out=acc,
+                lhsT=stationary[0][:, stationary_cols].bitcast(stationary_fmt),
+                lhsT_scale=stationary[1][:, stationary_cols],
+                rhs=moving[0][:, moving_cols].bitcast(E4M3),
+                rhs_scale=moving[1][:, moving_cols],
+                start=start,
+                stop=stop,
+            )
+
         offsets = sb.tile([P, SLOTS // 16], U16, name="offsets")
         wl_rows = wl.rearrange("(p t) c -> t p c", t=PACK)
         wm_rows = wm.rearrange("(p t) c -> t p c", t=PACK)
         wl_win = [f32_tile("wl_win%d" % t, POOL) for t in range(PACK)]
-        wm_win = [
-            sb.tile([P, POOL], F32, tag="wm_bytes%d" % t, name="wm_win%d" % t, align_bytes=64) for t in range(PACK)
-        ]
+        wm_win = [f32_on("wm_bytes%d" % t, "wm_win%d" % t, POOL) for t in range(PACK)]
         x_raw = f32_tile("x_raw", PACK * R)
-        tl_win = sb.tile([P, POOL], F32, tag="tl_bytes", name="tl_win", align_bytes=64)
-        tm_win = sb.tile([P, POOL], F32, tag="tm_bytes", name="tm_win", align_bytes=64)
+        tl_win = f32_on("tl_bytes", "tl_win", POOL)
+        tm_win = f32_on("tm_bytes", "tm_win", POOL)
         nc.sync.dma_start(offsets[:], offs)
         nc.sync.dma_start(tl_win[P - 1 : P, :], tl[0:1, :])
         nc.sync.dma_start(tm_win[P - 1 : P, :], tm[0:1, :])
-        row_vals = {}
-        for name, src in (("us", us), ("y", y), ("wt", wt)):
-            row_vals[name] = f32_tile(name + "_cols", PACK)
-            nc.scalar.dma_start(row_vals[name][:], src.rearrange("(s j) o -> s (j o)", j=PACK))
-        us_c, y_c, wt_c = row_vals["us"], row_vals["y"], row_vals["wt"]
+
+        def load_row_values(name, src):
+            cols = f32_tile(name, PACK)
+            nc.scalar.dma_start(cols[:], src.rearrange("(s j) o -> s (j o)", j=PACK))
+            return cols
+
+        us_cols = load_row_values("us_cols", us)
+        y_cols = load_row_values("y_cols", y)
+        wt_cols = load_row_values("wt_cols", wt)
         nc.sync.dma_start(x_raw[:], xT.rearrange("(p t) r -> p (t r)", t=PACK))
         for t in range(PACK):
             nc.sync.dma_start(wl_win[t][:], wl_rows[t])
@@ -92,65 +113,35 @@ def tile_attend_gmdn_x_pl_kernel(tc, xT, wl, wm, y, us, tl, tm, wt, offs, out_0,
             nc.scalar.activation(neg[:], src, ACT.Copy, scale=-1.0)
             return neg
 
-        neg_us = negated("neg_us", us_c[:])
-        neg_y = negated("neg_y", y_c[:])
+        neg_us = negated("neg_us", us_cols[:])
+        neg_y = negated("neg_y", y_cols[:])
         wu = f32_tile("wu", PACK)
-        nc.vector.tensor_tensor(wu[:], wt_c[:], us_c[:], ALU.mult)
+        nc.vector.tensor_tensor(wu[:], wt_cols[:], us_cols[:], ALU.mult)
         neg_wu = negated("neg_wu", wu[:])
 
         def gather_scales(name, window):
-            picked = f32_tile(name + "_picked")
+            picked = f32_tile(name, SLOTS)
             nc.vector.tensor_copy(picked[:], window[:].indirect(offsets[:]))
             return picked
 
-        def turn_scales(name, blocks):
-            turned = turn_bank(name + "_turned")
-            for u in range(PACK):
-                nc.tensor.transpose(turned[:, u * P : (u + 1) * P], blocks[u], ident[:])
-            return turned[:, P - 1 : PACK * P : P]
+        def turn_scales(name, pieces):
+            turned = turn_bank(name)
+            for n in range(PACK):
+                nc.tensor.transpose(turned[:, block(n)], pieces[n], ident[:])
+            return turned[:, P - 1 : BANK : P]
 
-        def gather_planes(name, windows):
-            planes = bf16_tile(name + "_planes", PACK * SLOTS)
-            for t in range(PACK):
-                nc.vector.tensor_copy(planes[:, t * SLOTS : (t + 1) * SLOTS], windows[t][:].indirect(offsets[:]))
-            return planes
+        tl_picked = gather_scales("tl_picked", tl_win)
+        tl_by_block = f32_tile("tl_by_block", PACK)
+        nc.scalar.copy(tl_by_block[:], turn_scales("tl_blocks", [tl_picked[:, block(k)] for k in range(PACK)]))
+        neg_tl_by_word = negated("neg_tl_by_word", turn_scales("tl_words", [tl_picked[:, u:SLOTS:PACK] for u in range(PACK)]))
 
-        def quantize_along_d(name, planes, vector_share):
-            grouped = bf16_tile(name + "_by_d", PACK * SLOTS)
-            dst = grouped[:].rearrange("p (c i t) -> p c t i", i=4, t=PACK)
-            src = planes[:].rearrange("p (t c i) -> p c t i", i=4, t=PACK)
-            if vector_share:
-                nc.vector.tensor_copy(dst[:, :vector_share], src[:, :vector_share])
-            nc.scalar.copy(dst[:, vector_share:], src[:, vector_share:])
-            return quantize(name + "_d", grouped[:], E4)
-
-        def quantize_along_slots(name, planes):
-            words = planes[:].bitcast(F32)
-            half = SLOTS // 2
-            grouped = bf16_tile(name + "_by_slot", PACK * D)
-            grouped_words = grouped[:].bitcast(F32).rearrange("s (p h k) -> s p h k", h=2, k=4)
-            for h in range(2):
-                turned = turn_bank("%s_turned%d" % (name, h))
-                for k in range(4):
-                    t, v = 2 * h + k // 2, k % 2
-                    nc.tensor.transpose(
-                        turned[:, k * P : (k + 1) * P], words[:, t * half + v : (t + 1) * half : 2], ident[:]
-                    )
-                nc.scalar.copy(grouped_words[:, :, h, :], turned[:].rearrange("s (k p) -> s p k", k=4))
-            return quantize(name + "_i", grouped[:], E4)
-
-        tl_picked = gather_scales("tl", tl_win)
-        tl_cols = f32_tile("tl_cols", PACK)
-        nc.scalar.copy(tl_cols[:], turn_scales("tl_runs", [tl_picked[:, k * P : (k + 1) * P] for k in range(PACK)]))
-        neg_tl_dealt = negated("neg_tl_dealt", turn_scales("tl_dealt", [tl_picked[:, u:SLOTS:PACK] for u in range(PACK)]))
-
-        tm_picked = gather_scales("tm", tm_win)
-        tm_cols = f32_tile("tm_cols", PACK)
-        nc.scalar.copy(tm_cols[:], turn_scales("tm_runs", [tm_picked[:, k * P : (k + 1) * P] for k in range(PACK)]))
+        tm_picked = gather_scales("tm_picked", tm_win)
+        tm_by_block = f32_tile("tm_by_block", PACK)
+        nc.scalar.copy(tm_by_block[:], turn_scales("tm_blocks", [tm_picked[:, block(k)] for k in range(PACK)]))
         tm_spread = turn_bank("tm_spread")
         for k in range(PACK):
-            nc.tensor.transpose(tm_spread[:, k * P : (k + 1) * P], tm_cols[:, k : k + 1].to_broadcast([P, P]), ident[:])
-        tm_rows = f32_tile("tm_rows")
+            nc.tensor.transpose(tm_spread[:, block(k)], tm_by_block[:, k : k + 1].to_broadcast([P, P]), ident[:])
+        tm_rows = f32_tile("tm_rows", SLOTS)
         nc.scalar.copy(tm_rows[:], tm_spread[:])
 
         x_grouped = bf16_tile("x_grouped", PACK * R)
@@ -158,28 +149,92 @@ def tile_attend_gmdn_x_pl_kernel(tc, xT, wl, wm, y, us, tl, tm, wt, offs, out_0,
             x_grouped[:].rearrange("p (j s t) -> p s t j", j=PACK, t=PACK),
             x_raw[:].rearrange("p (t s j) -> p s t j", j=PACK, t=PACK),
         )
-        x_codes, x_scales = quantize("x", x_grouped[:], E4)
+        x_q = quantize("x", x_grouped[:], E4M3)
 
-        wl_planes = gather_planes("wl", wl_win)
-        wl_d_codes, wl_d_scales = quantize_along_d("wl", wl_planes, 80)
-        wl_i_codes, wl_i_scales = quantize_along_slots("wl", wl_planes)
+        def gather_planes(name, windows):
+            planes = bf16_tile(name + "_planes", PACK * SLOTS)
+            for t in range(PACK):
+                nc.vector.tensor_copy(planes[:, t * SLOTS : (t + 1) * SLOTS], windows[t][:].indirect(offsets[:]))
+            return planes
 
-        wm_planes = gather_planes("wm", wm_win)
-        wm_d_codes, wm_d_scales = quantize_along_d("wm", wm_planes, 80)
-
-        def mx_pass(acc, stationary, stationary_cols, stationary_fmt, moving, moving_cols, start, stop):
-            nc.tensor.matmul_mx(
-                out=acc,
-                lhsT=stationary[0][:, stationary_cols].bitcast(stationary_fmt),
-                lhsT_scale=stationary[1][:, stationary_cols],
-                rhs=moving[0][:, moving_cols].bitcast(E4),
-                rhs_scale=moving[1][:, moving_cols],
-                start=start,
-                stop=stop,
+        def run_views(grouped, planes):
+            return (
+                grouped[:].rearrange("p (c i t) -> p c t i", i=RUN, t=PACK),
+                planes[:].rearrange("p (t c i) -> p c t i", i=RUN, t=PACK),
             )
 
-        def block(n):
-            return slice(n * P, (n + 1) * P)
+        def quantize_along_d(name, planes):
+            grouped = bf16_tile(name + "_by_d", PACK * SLOTS)
+            dst, src = run_views(grouped, planes)
+            nc.vector.tensor_copy(dst[:, :TABLE_RUNS_ON_VECTOR], src[:, :TABLE_RUNS_ON_VECTOR])
+            nc.scalar.copy(dst[:, TABLE_RUNS_ON_VECTOR:], src[:, TABLE_RUNS_ON_VECTOR:])
+            return quantize(name + "_d", grouped[:], E4M3)
+
+        def quantize_along_slots(name, planes):
+            pairs = planes[:].bitcast(F32)
+            plane_pairs = SLOTS // 2
+            grouped = bf16_tile(name + "_by_slot", PACK * D)
+            grouped_pairs = grouped[:].bitcast(F32).rearrange("s (p h n) -> s p h n", h=2, n=4)
+            for h in range(2):
+                turned = turn_bank("%s_turned%d" % (name, h))
+                for n in range(4):
+                    t, v = 2 * h + n // 2, n % 2
+                    nc.tensor.transpose(
+                        turned[:, block(n)], pairs[:, t * plane_pairs + v : (t + 1) * plane_pairs : 2], ident[:]
+                    )
+                nc.scalar.copy(grouped_pairs[:, :, h, :], turned[:].rearrange("s (n p) -> s p n", n=4))
+            return quantize(name + "_i", grouped[:], E4M3)
+
+        wl_planes = gather_planes("wl", wl_win)
+        wl_by_d = quantize_along_d("wl", wl_planes)
+        wl_by_slot = quantize_along_slots("wl", wl_planes)
+        wm_planes = gather_planes("wm", wm_win)
+        wm_by_d = quantize_along_d("wm", wm_planes)
+        wm_by_slot = quantize_along_slots("wm", wm_planes)
+
+        scaled_a = f32_on("tl_bytes", "scaled_a", PACK * R)
+        prior_sums = f32_tile("prior_sums", PACK)
+        neg_l, prior_exp = {}, {}
+        for pair in range(2):
+            rows = block(2 * pair, 2)
+            for k0 in range(0, PACK, 2):
+                a_turned = score_bank("a%d_%d" % (pair, k0))
+                for n in range(2):
+                    mx_pass(a_turned[:, block(2 * n, 2)], wl_by_d, block(k0 + n), E4M3, x_q, rows, True, True)
+                for n in range(2):
+                    nc.scalar.activation(
+                        scaled_a[:, block(PACK * (k0 + n) + 2 * pair, 2)],
+                        a_turned[:, block(2 * n, 2)],
+                        ACT.Copy,
+                        scale=tl_by_block[:, k0 + n : k0 + n + 1],
+                    )
+            neg_l_pair = f32_on("wm_bytes%d" % (2 * pair + 1), "neg_l%d" % pair, 2 * SLOTS)
+            for n in range(2):
+                j = 2 * pair + n
+                a_rows = row_bank(j, "a_rows%d" % j)
+                for k in range(PACK):
+                    nc.tensor.transpose(a_rows[:, block(k)], scaled_a[:, block(PACK * k + j)], ident[:])
+                neg_l[j] = neg_l_pair[:, n * SLOTS : (n + 1) * SLOTS]
+                neg_m = f32_tile("neg_m%d" % j, 1)
+                nc.vector.tensor_scalar(
+                    neg_l[j], a_rows[:], neg_us[:, j : j + 1], None, ALU.mult, ALU.min, accum_out=neg_m[:]
+                )
+                prior_exp[j] = f32_tile("prior_exp%d" % j, SLOTS)
+                nc.scalar.activation(
+                    prior_exp[j][:], neg_l[j], ACT.Exp, bias=neg_m[:], scale=-1.0, accum_out=prior_sums[:, j : j + 1]
+                )
+        prior_inv = f32_tile("prior_inv", PACK)
+        nc.vector.reciprocal(prior_inv[:], prior_sums[:])
+        neg_c1 = f32_tile("neg_c1", PACK)
+        nc.vector.tensor_tensor(neg_c1[:], prior_inv[:], neg_wu[:], ALU.mult)
+
+        result = f32_on("tm_bytes", "result", PACK * D)
+        out_rows = out_0.rearrange("(s j) d -> j s d", j=PACK)
+        all_columns = slice(0, SLOTS)
+        last = PACK - 1
+        half = D // 2
+        grads = [bf16_tile("grads%d" % j, 2 * SLOTS) for j in range(PACK)]
+        mean, post_exp, post_sum, diff = {}, {}, {}, {}
 
         def add_turned(dealt, acc, expd, factor, first):
             nc.scalar.activation(
@@ -190,117 +245,94 @@ def tile_attend_gmdn_x_pl_kernel(tc, xT, wl, wm, y, us, tl, tm, wt, offs, out_0,
             )
             for u in range(PACK):
                 nc.tensor.matmul(
-                    acc[:, u * P : (u + 1) * P],
-                    dealt[:, u * P : (u + 1) * P],
+                    acc[:, block(u)],
+                    dealt[:, block(u)],
                     ident[:],
                     is_transpose=True,
                     start=(first and u == 0),
                     stop=(not first and u == PACK - 1),
                 )
 
-        x_q = (x_codes, x_scales)
-        everything = slice(0, SLOTS)
-        scaled_a = sb.tile([P, PACK * R], F32, tag="tl_bytes", name="scaled_a", align_bytes=64)
-        neg_l_pairs = [
-            sb.tile([P, 2 * SLOTS], F32, tag="wm_bytes%d" % (2 * h + 1), name="neg_l%d" % h, align_bytes=64)
-            for h in range(2)
-        ]
-        prior_sums = f32_tile("prior_sums", PACK)
-        neg_logits, prior_exps = [], []
-        for j in range(PACK):
-            a_turned = score_bank("a%d" % j)
-            for k in range(PACK):
-                mx_pass(a_turned[:, block(k)], (wl_d_codes, wl_d_scales), block(k), E4, x_q, block(j), True, True)
-            a_rows = turn_bank("a_rows%d" % j)
-            for k in range(PACK):
-                piece = scaled_a[:, block(PACK * j + k)]
-                nc.scalar.activation(piece, a_turned[:, block(k)], ACT.Copy, scale=tl_cols[:, k : k + 1])
-                nc.tensor.transpose(a_rows[:, block(k)], piece, ident[:])
-            neg_l = neg_l_pairs[j // 2][:, (j % 2) * SLOTS : (j % 2 + 1) * SLOTS]
-            neg_m = f32_tile("neg_m%d" % j, 1)
-            nc.vector.tensor_scalar(neg_l, a_rows[:], neg_us[:, j : j + 1], None, ALU.mult, ALU.min, accum_out=neg_m[:])
-            e = f32_tile("prior_exp%d" % j)
-            nc.scalar.activation(e[:], neg_l, ACT.Exp, bias=neg_m[:], scale=-1.0, accum_out=prior_sums[:, j : j + 1])
-            neg_logits.append(neg_l)
-            prior_exps.append(e)
-        prior_inv = f32_tile("prior_inv", PACK)
-        nc.vector.reciprocal(prior_inv[:], prior_sums[:])
-        neg_c1 = f32_tile("neg_c1", PACK)
-        nc.vector.tensor_tensor(neg_c1[:], prior_inv[:], neg_wu[:], ALU.mult)
-
-        wm_i_codes, wm_i_scales = quantize_along_slots("wm", wm_planes)
-
-        result = sb.tile([P, PACK * D], F32, tag="tm_bytes", name="result", align_bytes=64)
-        out_rows = out_0.rearrange("(s j) d -> j s d", j=PACK)
-        mean, post_exp, post_sum, c2, diff, q_tm, grads = {}, {}, {}, {}, {}, {}, {}
-
         def posterior(j):
             b = score_bank("b%d" % j)
-            mx_pass(b[:], x_q, block(j), E4, (wm_d_codes, wm_d_scales), everything, True, True)
-            mean[j] = f32_tile("mean%d" % j)
-            nc.vector.scalar_tensor_tensor(mean[j][:], b[:], us_c[:, j : j + 1], tm_rows[:], ALU.mult, ALU.mult)
+            mx_pass(b[:], x_q, block(j), E4M3, wm_by_d, all_columns, True, True)
+            mean[j] = f32_tile("mean%d" % j, SLOTS)
+            nc.vector.scalar_tensor_tensor(mean[j][:], b[:], us_cols[:, j : j + 1], tm_rows[:], ALU.mult, ALU.mult)
             q_sq = f32_ring("q_sq", "q_sq%d" % j)
             nc.scalar.activation(q_sq[:], mean[j][:], ACT.Square, bias=neg_y[:, j : j + 1])
-            neg_s = f32_tile("neg_s%d" % j)
-            nc.vector.scalar_tensor_tensor(neg_s[:], q_sq[:], 0.5, neg_logits[j], ALU.mult, ALU.add)
+            neg_s = f32_tile("neg_s%d" % j, SLOTS)
+            nc.vector.scalar_tensor_tensor(neg_s[:], q_sq[:], 0.5, neg_l[j], ALU.mult, ALU.add)
             neg_ms = f32_tile("neg_ms%d" % j, 1)
             nc.vector.tensor_reduce(neg_ms[:], neg_s[:], AXIS_X, ALU.min)
-            post_exp[j] = f32_tile("post_exp%d" % j)
+            post_exp[j] = f32_tile("post_exp%d" % j, SLOTS)
             post_sum[j] = f32_tile("post_sum%d" % j, 1)
             nc.scalar.activation(post_exp[j][:], neg_s[:], ACT.Exp, bias=neg_ms[:], scale=-1.0, accum_out=post_sum[j][:])
-            diff[j] = grad_bank(j, "diff%d" % j)
-            add_turned(f32_tile("prior_dealt%d" % j), diff[j], prior_exps[j], neg_c1[:, j : j + 1], True)
+            diff[j] = row_bank(j, "diff%d" % j)
+            add_turned(f32_tile("prior_dealt%d" % j, SLOTS), diff[j], prior_exp[j], neg_c1[:, j : j + 1], True)
 
         def normalise(j):
-            inv = f32_tile("post_inv%d" % j, 1)
-            nc.vector.reciprocal(inv[:], post_sum[j][:])
-            c2[j] = f32_tile("c2_%d" % j, 1)
-            nc.scalar.activation(c2[j][:], inv[:], ACT.Copy, scale=wu[:, j : j + 1])
-            add_turned(f32_ring("post_dealt", "post_dealt%d" % j), diff[j], post_exp[j], c2[j][:], False)
-            q_tm[j] = f32_tile("q_tm%d" % j)
-            nc.vector.scalar_tensor_tensor(q_tm[j][:], mean[j][:], neg_y[:, j : j + 1], tm_rows[:], ALU.add, ALU.mult)
-
-        def gradients(j):
+            post_inv = f32_tile("post_inv%d" % j, 1)
+            nc.vector.reciprocal(post_inv[:], post_sum[j][:])
+            c2 = f32_tile("c2_%d" % j, 1)
+            nc.scalar.activation(c2[:], post_inv[:], ACT.Copy, scale=wu[:, j : j + 1])
+            add_turned(f32_ring("post_dealt", "post_dealt%d" % j), diff[j], post_exp[j], c2[:], False)
+            q_tm = f32_tile("q_tm%d" % j, SLOTS)
+            nc.vector.scalar_tensor_tensor(q_tm[:], mean[j][:], neg_y[:, j : j + 1], tm_rows[:], ALU.add, ALU.mult)
             gm = bf16_tile("gm%d" % j, SLOTS)
-            nc.vector.scalar_tensor_tensor(gm[:], post_exp[j][:], c2[j][:], q_tm[j][:], ALU.mult, ALU.mult)
+            nc.vector.scalar_tensor_tensor(gm[:], post_exp[j][:], c2[:], q_tm[:], ALU.mult, ALU.mult)
             gm_turned = turn_bank("gm_turned%d" % j)
             for v in range(2):
                 nc.tensor.transpose(gm_turned[:, block(v)], gm[:].bitcast(F32)[:, v : SLOTS // 2 : 2], ident[:])
-            grads[j] = bf16_tile("grads%d" % j, 2 * SLOTS)
             nc.scalar.copy(
-                grads[j][:].bitcast(F32)[:, SLOTS // 2 : SLOTS].rearrange("s (r v) -> s r v", v=2),
-                gm_turned[:, 0 : 2 * P].rearrange("s (v r) -> s r v", v=2),
-            )
-            nc.vector.tensor_tensor(
-                grads[j][:, 0:SLOTS].rearrange("s (r u) -> s r u", u=PACK),
-                diff[j][:].rearrange("s (u r) -> s r u", u=PACK),
-                neg_tl_dealt[:].unsqueeze(1).to_broadcast([P, P, PACK]),
-                ALU.mult,
+                grads[j][:].bitcast(F32)[:, 0 : SLOTS // 2].rearrange("s (r v) -> s r v", v=2),
+                gm_turned[:, block(0, 2)].rearrange("s (v r) -> s r v", v=2),
             )
 
         def back_product(j):
-            g_q = quantize("grads%d" % j, grads[j][:], E5)
-            acc = grad_bank(j, "x%d" % j)
-            mx_pass(acc[:], g_q, block(0), E5, (wl_i_codes, wl_i_scales), everything, True, False)
-            mx_pass(acc[:], g_q, block(1), E5, (wm_i_codes, wm_i_scales), everything, False, True)
-            nc.scalar.copy(result[:, j * D : (j + 1) * D], acc[:])
+            nc.vector.tensor_tensor(
+                grads[j][:, SLOTS:].rearrange("s (r u) -> s r u", u=PACK),
+                diff[j][:].rearrange("s (u r) -> s r u", u=PACK),
+                neg_tl_by_word[:].unsqueeze(1).to_broadcast([P, P, PACK]),
+                ALU.mult,
+            )
+            if j == last:
+                gm_q = quantize("gm%d" % j, grads[j][:, :SLOTS], E5M2)
+                gl_q = quantize("gl%d" % j, grads[j][:, SLOTS:], E5M2)
+                gl_cols, acc, piece = block(0), score_bank("x%d" % j), half
+            else:
+                gm_q = gl_q = quantize("grads%d" % j, grads[j][:], E5M2)
+                gl_cols, acc, piece = block(1), row_bank(j, "x%d" % j), D
+            mx_pass(acc[:], gm_q, block(0), E5M2, wm_by_slot, all_columns, True, False)
+            mx_pass(acc[:], gl_q, gl_cols, E5M2, wl_by_slot, all_columns, False, True)
+            for lo in range(0, D, piece):
+                nc.scalar.copy(result[:, j * D + lo : j * D + lo + piece], acc[:, lo : lo + piece])
             nc.sync.dma_start(out_rows[j], result[:, j * D : (j + 1) * D])
 
-        stages = (posterior, normalise, gradients, back_product)
+        stages = (posterior, normalise, back_product)
         for step in range(PACK + len(stages) - 1):
             for lag, stage in enumerate(stages):
                 if 0 <= step - lag < PACK:
                     stage(step - lag)
 
         result_grouped = bf16_tile("result_grouped", PACK * D)
-        dst = result_grouped[:].rearrange("p (c i j) -> p c j i", i=4, j=PACK)
-        src = result[:].rearrange("p (j c i) -> p c j i", i=4, j=PACK)
-        nc.vector.tensor_copy(dst[:, :96], src[:, :96])
-        nc.scalar.copy(dst[:, 96:], src[:, 96:])
-        r_codes, r_scales = quantize("result", result_grouped[:], E4)
-        nc.sync.dma_start(out_1[0].rearrange("p c l -> p (c l)").bitcast(I32), r_codes[:].bitcast(I32))
-        for quad in range(4):
-            queue = nc.scalar if quad % 2 else nc.sync
+        dst, src = run_views(result_grouped, result)
+        half_runs = half // RUN
+        nc.vector.tensor_copy(dst[:, :half_runs], src[:, :half_runs])
+        nc.vector.tensor_copy(dst[:, half_runs:RESULT_RUNS_ON_VECTOR], src[:, half_runs:RESULT_RUNS_ON_VECTOR])
+        nc.scalar.copy(dst[:, RESULT_RUNS_ON_VECTOR:], src[:, RESULT_RUNS_ON_VECTOR:])
+        result_codes = sb.tile([P, D], U32, name="result_codes", align_bytes=64)
+        result_scales = sb.tile([P, D], U8, name="result_scales", align_bytes=64)
+        out_words = out_1[0].rearrange("p c l -> p (c l)").bitcast(I32)
+        for lo in range(0, D, half):
+            cols = slice(lo, lo + half)
+            nc.vector.quantize_mx(
+                out=result_codes[:, cols].bitcast(E4M3),
+                scales=result_scales[:, cols],
+                in_=result_grouped[:, PACK * lo : PACK * (lo + half)],
+            )
+            nc.sync.dma_start(out_words[:, cols], result_codes[:, cols].bitcast(I32))
+        for n in range(4):
+            queue = nc.sync if n == 0 else nc.scalar
             queue.dma_start(
-                out_2[0, 4 * quad : 4 * quad + 4, :].bitcast(I32), r_scales[32 * quad : 32 * quad + 4, :].bitcast(I32)
+                out_2[0, 4 * n : 4 * n + 4, :].bitcast(I32), result_scales[32 * n : 32 * n + 4, :].bitcast(I32)
             )

@@ -85,9 +85,10 @@ def tile_attend_gmdn_x_pl_kernel(tc, xT, wl, wm, y, us, tl, tm, wt, offs, out_0,
         x_raw = f32_tile("x_raw", PACK * R)
         tl_win = f32_on("tl_bytes", "tl_win", POOL)
         tm_win = f32_on("tm_bytes", "tm_win", POOL)
+        nc.sync.dma_start(x_raw[:], xT.rearrange("(p t) r -> p (t r)", t=PACK))
+        nc.scalar.dma_start(tl_win[P - 1 : P, :], tl[0:1, :])
+        nc.scalar.dma_start(tm_win[P - 1 : P, :], tm[0:1, :])
         nc.sync.dma_start(offsets[:], offs)
-        nc.sync.dma_start(tl_win[P - 1 : P, :], tl[0:1, :])
-        nc.sync.dma_start(tm_win[P - 1 : P, :], tm[0:1, :])
 
         def load_row_values(name, src):
             cols = f32_tile(name, PACK)
@@ -97,7 +98,6 @@ def tile_attend_gmdn_x_pl_kernel(tc, xT, wl, wm, y, us, tl, tm, wt, offs, out_0,
         us_cols = load_row_values("us_cols", us)
         y_cols = load_row_values("y_cols", y)
         wt_cols = load_row_values("wt_cols", wt)
-        nc.sync.dma_start(x_raw[:], xT.rearrange("(p t) r -> p (t r)", t=PACK))
         for t in range(PACK):
             nc.sync.dma_start(wl_win[t][:], wl_rows[t])
         for t in range(PACK):
@@ -134,6 +134,11 @@ def tile_attend_gmdn_x_pl_kernel(tc, xT, wl, wm, y, us, tl, tm, wt, offs, out_0,
         tl_by_block = f32_tile("tl_by_block", PACK)
         nc.scalar.copy(tl_by_block[:], turn_scales("tl_blocks", [tl_picked[:, block(k)] for k in range(PACK)]))
         neg_tl_by_word = negated("neg_tl_by_word", turn_scales("tl_words", [tl_picked[:, u:SLOTS:PACK] for u in range(PACK)]))
+        neg_tl_grouped = f32_tile("neg_tl_grouped", SLOTS)
+        nc.scalar.copy(
+            neg_tl_grouped[:].rearrange("s (r u) -> s r u", u=PACK),
+            neg_tl_by_word[:].unsqueeze(1).to_broadcast([P, P, PACK]),
+        )
 
         tm_picked = gather_scales("tm_picked", tm_win)
         tm_by_block = f32_tile("tm_by_block", PACK)
@@ -292,7 +297,7 @@ def tile_attend_gmdn_x_pl_kernel(tc, xT, wl, wm, y, us, tl, tm, wt, offs, out_0,
             nc.vector.tensor_tensor(
                 grads[j][:, SLOTS:].rearrange("s (r u) -> s r u", u=PACK),
                 diff[j][:].rearrange("s (u r) -> s r u", u=PACK),
-                neg_tl_by_word[:].unsqueeze(1).to_broadcast([P, P, PACK]),
+                neg_tl_grouped[:].rearrange("s (r u) -> s r u", u=PACK),
                 ALU.mult,
             )
             if j == last:

from contextlib import ExitStack

import concourse.mybir as mybir
from concourse.masks import make_identity

F32 = mybir.dt.float32
BF16 = mybir.dt.bfloat16
I32 = mybir.dt.int32
U32 = mybir.dt.uint32
U16 = mybir.dt.uint16
U8 = mybir.dt.uint8
E4M3 = mybir.dt.float8_e4m3fn_x4
E5M2 = mybir.dt.float8_e5m2_x4
ALU = mybir.AluOpType
ACT = mybir.ActivationFunctionType
AXIS_X = mybir.AxisListType.X

P = 128
PACK = 4
D = 512
R = 512
SLOTS = 512
POOL = 2048
BANK = 512
RUN = 4
TABLE_RUNS_ON_VECTOR = 80
RESULT_RUNS_ON_VECTOR = 96
FLOPS = 4 * 2 * D * R * SLOTS


def block(n, count=1):
    return slice(n * P, (n + count) * P)


def tile_attend_gmdn_x_pl_kernel(tc, xT, wl, wm, y, us, tl, tm, wt, offs, out_0, out_1, out_2):
    nc = tc.nc
    with ExitStack() as ctx:
        sb = ctx.enter_context(tc.tile_pool(name="sb", bufs=1))
        ps = ctx.enter_context(tc.psum_pool(name="ps", bufs=1))

        def turn_bank(name):
            return ps.tile([P, BANK], F32, tag="turn", bufs=2, name=name)

        def score_bank(name):
            return ps.tile([P, BANK], F32, tag="score", bufs=2, name=name)

        def row_bank(j, name):
            return ps.tile([P, BANK], F32, tag="row%d" % j, bufs=1, name=name)

        def f32_tile(name, width):
            return sb.tile([P, width], F32, name=name, align_bytes=64)

        def f32_on(tag, name, width):
            return sb.tile([P, width], F32, tag=tag, name=name, align_bytes=64)

        def f32_ring(tag, name):
            return sb.tile([P, SLOTS], F32, tag=tag, bufs=2, name=name, align_bytes=64)

        def bf16_tile(name, width):
            return sb.tile([P, width], BF16, name=name, align_bytes=64)

        def quantize(name, grouped, fmt):
            width = grouped.shape[1] // PACK
            codes = sb.tile([P, width], U32, name=name + "_codes", align_bytes=64)
            scales = sb.tile([P, width], U8, name=name + "_scales", align_bytes=64)
            nc.vector.quantize_mx(out=codes[:].bitcast(fmt), scales=scales[:], in_=grouped)
            return codes, scales

        def mx_pass(acc, stationary, stationary_cols, stationary_fmt, moving, moving_cols, start, stop):
            nc.tensor.matmul_mx(
                out=acc,
                lhsT=stationary[0][:, stationary_cols].bitcast(stationary_fmt),
                lhsT_scale=stationary[1][:, stationary_cols],
                rhs=moving[0][:, moving_cols].bitcast(E4M3),
                rhs_scale=moving[1][:, moving_cols],
                start=start,
                stop=stop,
            )

        offsets = sb.tile([P, SLOTS // 16], U16, name="offsets")
        wl_rows = wl.rearrange("(p t) c -> t p c", t=PACK)
        wm_rows = wm.rearrange("(p t) c -> t p c", t=PACK)
        wl_win = [f32_tile("wl_win%d" % t, POOL) for t in range(PACK)]
        wm_win = [f32_on("wm_bytes%d" % t, "wm_win%d" % t, POOL) for t in range(PACK)]
        x_raw = f32_tile("x_raw", PACK * R)
        tl_win = f32_on("tl_bytes", "tl_win", POOL)
        tm_win = f32_on("tm_bytes", "tm_win", POOL)
        nc.sync.dma_start(x_raw[:], xT.rearrange("(p t) r -> p (t r)", t=PACK))
        nc.scalar.dma_start(tl_win[P - 1 : P, :], tl[0:1, :])
        nc.scalar.dma_start(tm_win[P - 1 : P, :], tm[0:1, :])
        nc.sync.dma_start(offsets[:], offs)

        def load_row_values(name, src):
            cols = f32_tile(name, PACK)
            nc.scalar.dma_start(cols[:], src.rearrange("(s j) o -> s (j o)", j=PACK))
            return cols

        us_cols = load_row_values("us_cols", us)
        y_cols = load_row_values("y_cols", y)
        wt_cols = load_row_values("wt_cols", wt)
        for t in range(PACK):
            nc.sync.dma_start(wl_win[t][:], wl_rows[t])
        for t in range(PACK):
            nc.sync.dma_start(wm_win[t][:], wm_rows[t])

        ident = f32_tile("ident", P)
        make_identity(nc, ident[:])
        nc.vector.memset(tl_win[0 : P - 1, :].bitcast(I32), 0)
        nc.gpsimd.memset(tm_win[0 : P - 1, :], 0.0)

        def negated(name, src):
            neg = f32_tile(name, PACK)
            nc.scalar.activation(neg[:], src, ACT.Copy, scale=-1.0)
            return neg

        neg_us = negated("neg_us", us_cols[:])
        neg_y = negated("neg_y", y_cols[:])
        wu = f32_tile("wu", PACK)
        nc.vector.tensor_tensor(wu[:], wt_cols[:], us_cols[:], ALU.mult)
        neg_wu = negated("neg_wu", wu[:])

        def gather_scales(name, window):
            picked = f32_tile(name, SLOTS)
            nc.vector.tensor_copy(picked[:], window[:].indirect(offsets[:]))
            return picked

        def turn_scales(name, pieces):
            turned = turn_bank(name)
            for n in range(PACK):
                nc.tensor.transpose(turned[:, block(n)], pieces[n], ident[:])
            return turned[:, P - 1 : BANK : P]

        tl_picked = gather_scales("tl_picked", tl_win)
        tl_by_block = f32_tile("tl_by_block", PACK)
        nc.scalar.copy(tl_by_block[:], turn_scales("tl_blocks", [tl_picked[:, block(k)] for k in range(PACK)]))
        neg_tl_by_word = negated("neg_tl_by_word", turn_scales("tl_words", [tl_picked[:, u:SLOTS:PACK] for u in range(PACK)]))
        neg_tl_grouped = f32_tile("neg_tl_grouped", SLOTS)
        nc.scalar.copy(
            neg_tl_grouped[:].rearrange("s (r u) -> s r u", u=PACK),
            neg_tl_by_word[:].unsqueeze(1).to_broadcast([P, P, PACK]),
        )

        tm_picked = gather_scales("tm_picked", tm_win)
        tm_by_block = f32_tile("tm_by_block", PACK)
        nc.scalar.copy(tm_by_block[:], turn_scales("tm_blocks", [tm_picked[:, block(k)] for k in range(PACK)]))
        tm_spread = turn_bank("tm_spread")
        for k in range(PACK):
            nc.tensor.transpose(tm_spread[:, block(k)], tm_by_block[:, k : k + 1].to_broadcast([P, P]), ident[:])
        tm_rows = f32_tile("tm_rows", SLOTS)
        nc.scalar.copy(tm_rows[:], tm_spread[:])

        x_grouped = bf16_tile("x_grouped", PACK * R)
        nc.vector.tensor_copy(
            x_grouped[:].rearrange("p (j s t) -> p s t j", j=PACK, t=PACK),
            x_raw[:].rearrange("p (t s j) -> p s t j", j=PACK, t=PACK),
        )
        x_q = quantize("x", x_grouped[:], E4M3)

        def gather_planes(name, windows):
            planes = bf16_tile(name + "_planes", PACK * SLOTS)
            for t in range(PACK):
                nc.vector.tensor_copy(planes[:, t * SLOTS : (t + 1) * SLOTS], windows[t][:].indirect(offsets[:]))
            return planes

        def run_views(grouped, planes):
            return (
                grouped[:].rearrange("p (c i t) -> p c t i", i=RUN, t=PACK),
                planes[:].rearrange("p (t c i) -> p c t i", i=RUN, t=PACK),
            )

        def quantize_along_d(name, planes):
            grouped = bf16_tile(name + "_by_d", PACK * SLOTS)
            dst, src = run_views(grouped, planes)
            nc.vector.tensor_copy(dst[:, :TABLE_RUNS_ON_VECTOR], src[:, :TABLE_RUNS_ON_VECTOR])
            nc.scalar.copy(dst[:, TABLE_RUNS_ON_VECTOR:], src[:, TABLE_RUNS_ON_VECTOR:])
            return quantize(name + "_d", grouped[:], E4M3)

        def quantize_along_slots(name, planes):
            pairs = planes[:].bitcast(F32)
            plane_pairs = SLOTS // 2
            grouped = bf16_tile(name + "_by_slot", PACK * D)
            grouped_pairs = grouped[:].bitcast(F32).rearrange("s (p h n) -> s p h n", h=2, n=4)
            for h in range(2):
                turned = turn_bank("%s_turned%d" % (name, h))
                for n in range(4):
                    t, v = 2 * h + n // 2, n % 2
                    nc.tensor.transpose(
                        turned[:, block(n)], pairs[:, t * plane_pairs + v : (t + 1) * plane_pairs : 2], ident[:]
                    )
                nc.scalar.copy(grouped_pairs[:, :, h, :], turned[:].rearrange("s (n p) -> s p n", n=4))
            return quantize(name + "_i", grouped[:], E4M3)

        wl_planes = gather_planes("wl", wl_win)
        wl_by_d = quantize_along_d("wl", wl_planes)
        wl_by_slot = quantize_along_slots("wl", wl_planes)
        wm_planes = gather_planes("wm", wm_win)
        wm_by_d = quantize_along_d("wm", wm_planes)
        wm_by_slot = quantize_along_slots("wm", wm_planes)

        scaled_a = f32_on("tl_bytes", "scaled_a", PACK * R)
        prior_sums = f32_tile("prior_sums", PACK)
        neg_l, prior_exp = {}, {}
        for pair in range(2):
            rows = block(2 * pair, 2)
            for k0 in range(0, PACK, 2):
                a_turned = score_bank("a%d_%d" % (pair, k0))
                for n in range(2):
                    mx_pass(a_turned[:, block(2 * n, 2)], wl_by_d, block(k0 + n), E4M3, x_q, rows, True, True)
                for n in range(2):
                    nc.scalar.activation(
                        scaled_a[:, block(PACK * (k0 + n) + 2 * pair, 2)],
                        a_turned[:, block(2 * n, 2)],
                        ACT.Copy,
                        scale=tl_by_block[:, k0 + n : k0 + n + 1],
                    )
            neg_l_pair = f32_on("wm_bytes%d" % (2 * pair + 1), "neg_l%d" % pair, 2 * SLOTS)
            for n in range(2):
                j = 2 * pair + n
                a_rows = row_bank(j, "a_rows%d" % j)
                for k in range(PACK):
                    nc.tensor.transpose(a_rows[:, block(k)], scaled_a[:, block(PACK * k + j)], ident[:])
                neg_l[j] = neg_l_pair[:, n * SLOTS : (n + 1) * SLOTS]
                neg_m = f32_tile("neg_m%d" % j, 1)
                nc.vector.tensor_scalar(
                    neg_l[j], a_rows[:], neg_us[:, j : j + 1], None, ALU.mult, ALU.min, accum_out=neg_m[:]
                )
                prior_exp[j] = f32_tile("prior_exp%d" % j, SLOTS)
                nc.scalar.activation(
                    prior_exp[j][:], neg_l[j], ACT.Exp, bias=neg_m[:], scale=-1.0, accum_out=prior_sums[:, j : j + 1]
                )
        prior_inv = f32_tile("prior_inv", PACK)
        nc.vector.reciprocal(prior_inv[:], prior_sums[:])
        neg_c1 = f32_tile("neg_c1", PACK)
        nc.vector.tensor_tensor(neg_c1[:], prior_inv[:], neg_wu[:], ALU.mult)

        result = f32_on("tm_bytes", "result", PACK * D)
        out_rows = out_0.rearrange("(s j) d -> j s d", j=PACK)
        all_columns = slice(0, SLOTS)
        last = PACK - 1
        half = D // 2
        grads = [bf16_tile("grads%d" % j, 2 * SLOTS) for j in range(PACK)]
        mean, post_exp, post_sum, diff = {}, {}, {}, {}

        def add_turned(dealt, acc, expd, factor, first):
            nc.scalar.activation(
                dealt[:].rearrange("r (u s) -> r s u", u=PACK),
                expd[:].rearrange("r (s u) -> r s u", u=PACK),
                ACT.Copy,
                scale=factor,
            )
            for u in range(PACK):
                nc.tensor.matmul(
                    acc[:, block(u)],
                    dealt[:, block(u)],
                    ident[:],
                    is_transpose=True,
                    start=(first and u == 0),
                    stop=(not first and u == PACK - 1),
                )

        def posterior(j):
            b = score_bank("b%d" % j)
            mx_pass(b[:], x_q, block(j), E4M3, wm_by_d, all_columns, True, True)
            mean[j] = f32_tile("mean%d" % j, SLOTS)
            nc.vector.scalar_tensor_tensor(mean[j][:], b[:], us_cols[:, j : j + 1], tm_rows[:], ALU.mult, ALU.mult)
            q_sq = f32_ring("q_sq", "q_sq%d" % j)
            nc.scalar.activation(q_sq[:], mean[j][:], ACT.Square, bias=neg_y[:, j : j + 1])
            neg_s = f32_tile("neg_s%d" % j, SLOTS)
            nc.vector.scalar_tensor_tensor(neg_s[:], q_sq[:], 0.5, neg_l[j], ALU.mult, ALU.add)
            neg_ms = f32_tile("neg_ms%d" % j, 1)
            nc.vector.tensor_reduce(neg_ms[:], neg_s[:], AXIS_X, ALU.min)
            post_exp[j] = f32_tile("post_exp%d" % j, SLOTS)
            post_sum[j] = f32_tile("post_sum%d" % j, 1)
            nc.scalar.activation(post_exp[j][:], neg_s[:], ACT.Exp, bias=neg_ms[:], scale=-1.0, accum_out=post_sum[j][:])
            diff[j] = row_bank(j, "diff%d" % j)
            add_turned(f32_tile("prior_dealt%d" % j, SLOTS), diff[j], prior_exp[j], neg_c1[:, j : j + 1], True)

        def normalise(j):
            post_inv = f32_tile("post_inv%d" % j, 1)
            nc.vector.reciprocal(post_inv[:], post_sum[j][:])
            c2 = f32_tile("c2_%d" % j, 1)
            nc.scalar.activation(c2[:], post_inv[:], ACT.Copy, scale=wu[:, j : j + 1])
            add_turned(f32_ring("post_dealt", "post_dealt%d" % j), diff[j], post_exp[j], c2[:], False)
            q_tm = f32_tile("q_tm%d" % j, SLOTS)
            nc.vector.scalar_tensor_tensor(q_tm[:], mean[j][:], neg_y[:, j : j + 1], tm_rows[:], ALU.add, ALU.mult)
            gm = bf16_tile("gm%d" % j, SLOTS)
            nc.vector.scalar_tensor_tensor(gm[:], post_exp[j][:], c2[:], q_tm[:], ALU.mult, ALU.mult)
            gm_turned = turn_bank("gm_turned%d" % j)
            for v in range(2):
                nc.tensor.transpose(gm_turned[:, block(v)], gm[:].bitcast(F32)[:, v : SLOTS // 2 : 2], ident[:])
            nc.scalar.copy(
                grads[j][:].bitcast(F32)[:, 0 : SLOTS // 2].rearrange("s (r v) -> s r v", v=2),
                gm_turned[:, block(0, 2)].rearrange("s (v r) -> s r v", v=2),
            )

        def back_product(j):
            nc.vector.tensor_tensor(
                grads[j][:, SLOTS:].rearrange("s (r u) -> s r u", u=PACK),
                diff[j][:].rearrange("s (u r) -> s r u", u=PACK),
                neg_tl_grouped[:].rearrange("s (r u) -> s r u", u=PACK),
                ALU.mult,
            )
            if j == last:
                gm_q = quantize("gm%d" % j, grads[j][:, :SLOTS], E5M2)
                gl_q = quantize("gl%d" % j, grads[j][:, SLOTS:], E5M2)
                gl_cols, acc, piece = block(0), score_bank("x%d" % j), half
            else:
                gm_q = gl_q = quantize("grads%d" % j, grads[j][:], E5M2)
                gl_cols, acc, piece = block(1), row_bank(j, "x%d" % j), D
            mx_pass(acc[:], gm_q, block(0), E5M2, wm_by_slot, all_columns, True, False)
            mx_pass(acc[:], gl_q, gl_cols, E5M2, wl_by_slot, all_columns, False, True)
            for lo in range(0, D, piece):
                nc.scalar.copy(result[:, j * D + lo : j * D + lo + piece], acc[:, lo : lo + piece])
            nc.sync.dma_start(out_rows[j], result[:, j * D : (j + 1) * D])

        stages = (posterior, normalise, back_product)
        for step in range(PACK + len(stages) - 1):
            for lag, stage in enumerate(stages):
                if 0 <= step - lag < PACK:
                    stage(step - lag)

        result_grouped = bf16_tile("result_grouped", PACK * D)
        dst, src = run_views(result_grouped, result)
        half_runs = half // RUN
        nc.vector.tensor_copy(dst[:, :half_runs], src[:, :half_runs])
        nc.vector.tensor_copy(dst[:, half_runs:RESULT_RUNS_ON_VECTOR], src[:, half_runs:RESULT_RUNS_ON_VECTOR])
        nc.scalar.copy(dst[:, RESULT_RUNS_ON_VECTOR:], src[:, RESULT_RUNS_ON_VECTOR:])
        result_codes = sb.tile([P, D], U32, name="result_codes", align_bytes=64)
        result_scales = sb.tile([P, D], U8, name="result_scales", align_bytes=64)
        out_words = out_1[0].rearrange("p c l -> p (c l)").bitcast(I32)
        for lo in range(0, D, half):
            cols = slice(lo, lo + half)
            nc.vector.quantize_mx(
                out=result_codes[:, cols].bitcast(E4M3),
                scales=result_scales[:, cols],
                in_=result_grouped[:, PACK * lo : PACK * (lo + half)],
            )
            nc.sync.dma_start(out_words[:, cols], result_codes[:, cols].bitcast(I32))
        for n in range(4):
            queue = nc.sync if n == 0 else nc.scalar
            queue.dma_start(
                out_2[0, 4 * n : 4 * n + 4, :].bitcast(I32), result_scales[32 * n : 32 * n + 4, :].bitcast(I32)
            )
